import numpy as np, ml_dtypes
CORES = [30,158,46,174,86,214]
N = 6
C = 128
def setup_inputs(rng):
    x = rng.standard_normal((N, 128, C), dtype=np.float32) * (0.25 + np.abs(rng.standard_normal((N, 1, C), dtype=np.float32)))
    return {"x": x.astype(ml_dtypes.bfloat16)}
def setup_inputs_big(rng):
    d = setup_inputs(rng)
    for k in ("x",): d[k] = (d[k].astype(np.float32) * 1024.0).astype(d[k].dtype)
    return d
def setup_inputs_small(rng):
    d = setup_inputs(rng)
    for k in ("x",): d[k] = (d[k].astype(np.float32) * (1 / 1024.0)).astype(d[k].dtype)
    return d
def setup_inputs_apart(rng):
    d = setup_inputs(rng)
    f = (10.0 ** rng.permutation(np.linspace(-1.5, 1.5, N))).astype(np.float32).reshape(N, 1, 1)
    for k in ("x",): d[k] = (d[k].astype(np.float32) * f).astype(d[k].dtype)
    return d
def setup_inputs_mixed(rng):
    d = setup_inputs(rng)
    f = (10.0 ** rng.uniform(-3, 3, (N, 1, C))).astype(np.float32); shape = rng.integers(3, size=(N, 1, C))
    for k in ("x",):
        x = d[k].astype(np.float32)
        m = x.mean(axis=1, keepdims=True); level = m + np.sign(x - m) * np.abs(x - m).mean(axis=1, keepdims=True) * rng.uniform(0.9, 1.1, x.shape).astype(np.float32)
        other = x * np.where(rng.random(x.shape) < 0.016, 100.0, 1.0).astype(np.float32)
        d[k] = (np.where(shape == 1, level, np.where(shape == 2, other, x)) * f).astype(d[k].dtype)
    return d
def reference(x):
    X = x.astype(np.float64); U = X / np.sqrt((X ** 2).sum(axis=1, keepdims=True))
    y = np.full((N, C, N * C), np.nan)
    for r in range(N):
        for s in range(N):
            if s != r: y[r][:, C * s:C * s + C] = U[r].T @ U[s]
    return {"y": y.astype(ml_dtypes.bfloat16)}

@@ -1,0 +1,152 @@
+from concourse.bass import DstId, RemoteDMATransfer
+from concourse.mybir import AluOpType, ActivationFunctionType
+
+N = 6
+C = 128
+D_OFFS = [1, 2, 3]
+S_OFFS = [4, 5]
+PROC = [4, 1, 2, 5, 3]
+TINY = 2e-35
+
+SCRATCH = {
+    "land": ("sbuf", [128, N * C], "bfloat16"),
+    "sq": ("sbuf", [128, N * C], "bfloat16"),
+    "qs": ("sbuf", [128, N * C], "bfloat16"),
+    "yb": ("sbuf", [128, N * C], "bfloat16"),
+    "ones": ("sbuf", [128, 8], "bfloat16"),
+    "ident": ("sbuf", [128, C], "bfloat16"),
+    "ln": ("sbuf", [128, 8], "float32"),
+    "inv": ("sbuf", [128, 8], "float32"),
+    "xd": ("dram", [128, C], "bfloat16"),
+    "dl": ("dram", [N, 128, C], "bfloat16"),
+    "pq0": ("psum", [128, 512], "float32"),
+    "pq1": ("psum", [128, 512], "float32"),
+    "pq2": ("psum", [128, 512], "float32"),
+    "pq3": ("psum", [128, 512], "float32"),
+    "pq4": ("psum", [128, 512], "float32"),
+    "pown": ("psum", [128, 512], "float32"),
+    "pt0": ("psum", [128, 1024], "bfloat16"),
+    "pt1": ("psum", [128, 1024], "bfloat16"),
+}
+SEMAPHORES = (["ld", "ldd", "loc", "st", "c1", "c2", "idd", "pn"]
+              + ["%s%d" % (n, i) for n in ("arr", "rdy", "sqd", "srt", "rec") for i in range(N)]
+              + ["%s%d" % (n, i) for n in ("pe", "qsc", "tr", "fin") for i in range(N - 1)])
+
+
+def rank_program(g, core, T, topo):
+    r = T.rank_of(core)
+    if r is None:
+        return
+    A = ActivationFunctionType
+    sem = T.sem
+
+    def blk(t, s):
+        return t[:, s * C:(s + 1) * C]
+
+    def col(t, s):
+        return t[:, s:s + 1]
+
+    def kind(j):
+        return D_OFFS if j in D_OFFS else S_OFFS
+
+    def engines(s, offs):
+        m = topo.mask(T.cores[s], T.cores[(s + offs[0]) % N])
+        for j in offs:
+            m &= topo.mask(T.cores[s], T.cores[(s + j) % N])
+        return m
+
+    g.sync.dma_start(blk(T.land, r), T.x[:]).then_inc(sem.ld, 16)
+    if D_OFFS:
+        g.scalar.dma_start(T.xd[:], T.x[:]).then_inc(sem.ldd, 16)
+    g.vector.memset(T.ones[:], 1.0).then_inc(sem.c1, 1)
+    g.vector.memset(T.ident[:], 1.0).then_inc(sem.c2, 1)
+
+    def send(offs, src_ap, dst_ap):
+        m = engines(r, offs)
+        ids = []
+        for j in offs:
+            rid, pid = topo.addr(T.cores[(r + j) % N], core)
+            ids.append(DstId(rid=rid, pnc=pid))
+        g.remote_dma_fused([RemoteDMATransfer(dst_ids=ids, dma_engine_mask=m, remote_sem=sem["arr%d" % r],
+                                              srcs=[src_ap], dsts=[dst_ap] * len(offs), alu_op=0)], local_sem=sem.loc)
+        return bin(m).count("1")
+
+    left = 0
+    if D_OFFS:
+        g.wait_ge(sem.ldd, 16)
+        left += send(D_OFFS, T.xd[:], T.dl[r])
+    if S_OFFS:
+        g.wait_ge(sem.ld, 16)
+        left += send(S_OFFS, blk(T.land, r), blk(T.land, r))
+    g.wait_ge(sem.c2, 1)
+    g.affine_select(T.ident[:], T.ident[:], [[-1, C]], AluOpType.is_equal, 0.0, 0, 1).then_inc(sem.idd, 1)
+    g.wait_ge(sem.loc, left)
+
+    def arrived(j):
+        return bin(engines((r - j) % N, kind(j))).count("1")
+
+    src = [(r - j) % N for j in PROC]
+    ready = []
+    for j, s in zip(PROC, src):
+        ready.append((sem["rdy%d" % s], 16) if j in D_OFFS else (sem["arr%d" % s], arrived(j)))
+
+    g.scalar.wait_ge(sem.ld, 16)
+    g.scalar.activation(blk(T.sq, r), blk(T.land, r), A.Square).then_inc(sem["sqd%d" % r], 1)
+    g.tensor.wait_ge(sem["sqd%d" % r], 1)
+    g.tensor.wait_ge(sem.c1, 1)
+    g.tensor.wait_ge(sem.ld, 16)
+    g.tensor.matmul(T.pown[:, 0:1], blk(T.sq, r), T.ones[:, 0:1], True, True).then_inc(sem.pn, 1)
+    g.scalar.wait_ge(sem.pn, 1)
+    g.scalar.activation(col(T.ln, r), T.pown[:, 0:1], A.Sqrt, bias=TINY).then_inc(sem["srt%d" % r], 1)
+    g.vector.wait_ge(sem["srt%d" % r], 1)
+    g.vector.reciprocal(col(T.inv, r), col(T.ln, r)).then_inc(sem["rec%d" % r], 1)
+
+    for n, j in enumerate(D_OFFS):
+        s = (r - j) % N
+        q = g.sync if n % 2 == 0 else g.scalar
+        q.wait_ge(sem["arr%d" % s], arrived(j))
+        q.dma_start(blk(T.land, s), T.dl[s]).then_inc(sem["rdy%d" % s], 16)
+
+    pq = [T.pq0, T.pq1, T.pq2, T.pq3, T.pq4]
+    pt = [T.pt0, T.pt1]
+    last = N - 2
+
+    def turn(k):
+        g.tensor.wait_ge(sem["qsc%d" % k], 1)
+        if k == 0:
+            g.tensor.wait_ge(sem.idd, 1)
+        if k >= 2:
+            g.tensor.wait_ge(sem["fin%d" % (k - 2)], 1)
+        g.tensor.transpose(pt[k % 2][:, 0:C], blk(T.qs, src[k]), T.ident[:]).then_inc(sem["tr%d" % k], 1)
+
+    for k, s in enumerate(src):
+        rs, rn = ready[k]
+        g.tensor.wait_ge(rs, rn)
+        g.tensor.matmul(pq[k][:, 0:C], blk(T.land, s), blk(T.land, r), True, True).then_inc(sem["pe%d" % k], 1)
+        g.scalar.wait_ge(rs, rn)
+        g.scalar.activation(blk(T.sq, s), blk(T.land, s), A.Square).then_inc(sem["sqd%d" % s], 1)
+        g.tensor.wait_ge(sem["sqd%d" % s], 1)
+        g.tensor.matmul(pq[k][:, C:C + 1], blk(T.sq, s), T.ones[:, 0:1], True, True).then_inc(sem["pe%d" % k], 1)
+        g.scalar.wait_ge(sem["pe%d" % k], 2)
+        g.scalar.activation(col(T.ln, s), pq[k][:, C:C + 1], A.Sqrt, bias=TINY).then_inc(sem["srt%d" % s], 1)
+        g.vector.wait_ge(sem["srt%d" % s], 1)
+        g.vector.reciprocal(col(T.inv, s), col(T.ln, s)).then_inc(sem["rec%d" % s], 1)
+        g.vector.wait_ge(sem["rec%d" % s], 1)
+        g.vector.wait_ge(sem["pe%d" % k], 2)
+        g.vector.tensor_scalar(blk(T.qs, s), pq[k][:, 0:C], col(T.inv, s), None, AluOpType.mult).then_inc(sem["qsc%d" % k], 1)
+        if k >= 1:
+            turn(k - 1)
+            g.scalar.wait_ge(sem["tr%d" % (k - 1)], 1)
+            g.scalar.wait_ge(sem["rec%d" % r], 1)
+            g.scalar.activation(blk(T.yb, src[k - 1]), pt[(k - 1) % 2][:, 0:C], A.Copy,
+                                scale=col(T.inv, r)).then_inc(sem["fin%d" % (k - 1)], 1)
+    turn(last)
+    g.vector.wait_ge(sem["tr%d" % last], 1)
+    g.vector.wait_ge(sem["rec%d" % r], 1)
+    g.vector.tensor_scalar(blk(T.yb, src[last]), pt[last % 2][:, 0:C], col(T.inv, r), None,
+                           AluOpType.mult).then_inc(sem["fin%d" % last], 1)
+
+    for k, s in enumerate(src):
+        g.sync.wait_ge(sem["fin%d" % k], 1)
+        g.sync.dma_start(blk(T.y, s), blk(T.yb, s)).then_inc(sem.st, 16)
+    g.sync.wait_ge(sem.st, 16 * (N - 1))

@@ -3,9 +3,6 @@ from concourse.mybir import AluOpType, ActivationFunctionType
 
 N = 6
 C = 128
-D_OFFS = [1, 2, 3]
-S_OFFS = [4, 5]
-PROC = [4, 1, 2, 5, 3]
 TINY = 2e-35
 
 SCRATCH = {
@@ -17,8 +14,6 @@ SCRATCH = {
     "ident": ("sbuf", [128, C], "bfloat16"),
     "ln": ("sbuf", [128, 8], "float32"),
     "inv": ("sbuf", [128, 8], "float32"),
-    "xd": ("dram", [128, C], "bfloat16"),
-    "dl": ("dram", [N, 128, C], "bfloat16"),
     "pq0": ("psum", [128, 512], "float32"),
     "pq1": ("psum", [128, 512], "float32"),
     "pq2": ("psum", [128, 512], "float32"),
@@ -28,9 +23,31 @@ SCRATCH = {
     "pt0": ("psum", [128, 1024], "bfloat16"),
     "pt1": ("psum", [128, 1024], "bfloat16"),
 }
-SEMAPHORES = (["ld", "ldd", "loc", "st", "c1", "c2", "idd", "pn"]
-              + ["%s%d" % (n, i) for n in ("arr", "rdy", "sqd", "srt", "rec") for i in range(N)]
+SEMAPHORES = (["ld", "loc", "st", "c1", "c2", "idd", "pn"]
+              + ["%s%d" % (n, i) for n in ("arr", "sqd", "srt", "rec") for i in range(N)]
               + ["%s%d" % (n, i) for n in ("pe", "qsc", "tr", "fin") for i in range(N - 1)])
+
+
+def plan(near):
+    used = [[a == b for b in range(N)] for a in range(N)]
+    rounds = []
+    for _ in range(N - 1):
+        best = [None, -1]
+
+        def rec(a, perm, score):
+            if a == N:
+                if score > best[1]:
+                    best[0], best[1] = perm, score
+                return
+            for b in range(N):
+                if not used[a][b] and b not in perm:
+                    rec(a + 1, perm + [b], score + (1 if near[a][b] else 0))
+
+        rec(0, [], 0)
+        for a, b in enumerate(best[0]):
+            used[a][b] = True
+        rounds.insert(0, best[0])
+    return rounds
 
 
 def rank_program(g, core, T, topo):
@@ -46,49 +63,32 @@ def rank_program(g, core, T, topo):
     def col(t, s):
         return t[:, s:s + 1]
 
-    def kind(j):
-        return D_OFFS if j in D_OFFS else S_OFFS
-
-    def engines(s, offs):
-        m = topo.mask(T.cores[s], T.cores[(s + offs[0]) % N])
-        for j in offs:
-            m &= topo.mask(T.cores[s], T.cores[(s + j) % N])
+    def engines(s):
+        m = -1
+        for d in T.cores:
+            if d != T.cores[s]:
+                m &= topo.mask(T.cores[s], d)
         return m
 
+    rounds = plan([[a != b and topo.same_plane(T.cores[a], T.cores[b]) for b in range(N)] for a in range(N)])
+    peers = [rd[r] for rd in rounds]
+    src = [rd.index(r) for rd in rounds]
+
     g.sync.dma_start(blk(T.land, r), T.x[:]).then_inc(sem.ld, 16)
-    if D_OFFS:
-        g.scalar.dma_start(T.xd[:], T.x[:]).then_inc(sem.ldd, 16)
     g.vector.memset(T.ones[:], 1.0).then_inc(sem.c1, 1)
     g.vector.memset(T.ident[:], 1.0).then_inc(sem.c2, 1)
 
-    def send(offs, src_ap, dst_ap):
-        m = engines(r, offs)
-        ids = []
-        for j in offs:
-            rid, pid = topo.addr(T.cores[(r + j) % N], core)
-            ids.append(DstId(rid=rid, pnc=pid))
-        g.remote_dma_fused([RemoteDMATransfer(dst_ids=ids, dma_engine_mask=m, remote_sem=sem["arr%d" % r],
-                                              srcs=[src_ap], dsts=[dst_ap] * len(offs), alu_op=0)], local_sem=sem.loc)
-        return bin(m).count("1")
-
-    left = 0
-    if D_OFFS:
-        g.wait_ge(sem.ldd, 16)
-        left += send(D_OFFS, T.xd[:], T.dl[r])
-    if S_OFFS:
-        g.wait_ge(sem.ld, 16)
-        left += send(S_OFFS, blk(T.land, r), blk(T.land, r))
+    ids = []
+    for p in peers:
+        rid, pid = topo.addr(T.cores[p], core)
+        ids.append(DstId(rid=rid, pnc=pid))
+    g.wait_ge(sem.ld, 16)
+    g.remote_dma_fused([RemoteDMATransfer(dst_ids=ids, dma_engine_mask=engines(r), remote_sem=sem["arr%d" % r],
+                                          srcs=[blk(T.land, r)], dsts=[blk(T.land, r)] * len(ids), alu_op=0)],
+                       local_sem=sem.loc)
     g.wait_ge(sem.c2, 1)
     g.affine_select(T.ident[:], T.ident[:], [[-1, C]], AluOpType.is_equal, 0.0, 0, 1).then_inc(sem.idd, 1)
-    g.wait_ge(sem.loc, left)
-
-    def arrived(j):
-        return bin(engines((r - j) % N, kind(j))).count("1")
-
-    src = [(r - j) % N for j in PROC]
-    ready = []
-    for j, s in zip(PROC, src):
-        ready.append((sem["rdy%d" % s], 16) if j in D_OFFS else (sem["arr%d" % s], arrived(j)))
+    g.wait_ge(sem.loc, bin(engines(r)).count("1"))
 
     g.scalar.wait_ge(sem.ld, 16)
     g.scalar.activation(blk(T.sq, r), blk(T.land, r), A.Square).then_inc(sem["sqd%d" % r], 1)
@@ -100,12 +100,6 @@ def rank_program(g, core, T, topo):
     g.scalar.activation(col(T.ln, r), T.pown[:, 0:1], A.Sqrt, bias=TINY).then_inc(sem["srt%d" % r], 1)
     g.vector.wait_ge(sem["srt%d" % r], 1)
     g.vector.reciprocal(col(T.inv, r), col(T.ln, r)).then_inc(sem["rec%d" % r], 1)
-
-    for n, j in enumerate(D_OFFS):
-        s = (r - j) % N
-        q = g.sync if n % 2 == 0 else g.scalar
-        q.wait_ge(sem["arr%d" % s], arrived(j))
-        q.dma_start(blk(T.land, s), T.dl[s]).then_inc(sem["rdy%d" % s], 16)
 
     pq = [T.pq0, T.pq1, T.pq2, T.pq3, T.pq4]
     pt = [T.pt0, T.pt1]
@@ -120,7 +114,7 @@ def rank_program(g, core, T, topo):
         g.tensor.transpose(pt[k % 2][:, 0:C], blk(T.qs, src[k]), T.ident[:]).then_inc(sem["tr%d" % k], 1)
 
     for k, s in enumerate(src):
-        rs, rn = ready[k]
+        rs, rn = sem["arr%d" % s], bin(engines(s)).count("1")
         g.tensor.wait_ge(rs, rn)
         g.tensor.matmul(pq[k][:, 0:C], blk(T.land, s), blk(T.land, r), True, True).then_inc(sem["pe%d" % k], 1)
         g.scalar.wait_ge(rs, rn)

@@ -3,6 +3,7 @@ from concourse.mybir import AluOpType, ActivationFunctionType
 
 N = 6
 C = 128
+RAW = 3
 TINY = 2e-35
 
 SCRATCH = {
@@ -10,8 +11,10 @@ SCRATCH = {
     "sq": ("sbuf", [128, N * C], "bfloat16"),
     "qs": ("sbuf", [128, N * C], "bfloat16"),
     "yb": ("sbuf", [128, N * C], "bfloat16"),
-    "ones": ("sbuf", [128, 8], "bfloat16"),
+    "ones": ("sbuf", [128, C], "bfloat16"),
     "ident": ("sbuf", [128, C], "bfloat16"),
+    "dg": ("sbuf", [128, C], "bfloat16"),
+    "u": ("sbuf", [128, C], "bfloat16"),
     "ln": ("sbuf", [128, 8], "float32"),
     "inv": ("sbuf", [128, 8], "float32"),
     "pq0": ("psum", [128, 512], "float32"),
@@ -23,7 +26,7 @@ SCRATCH = {
     "pt0": ("psum", [128, 1024], "bfloat16"),
     "pt1": ("psum", [128, 1024], "bfloat16"),
 }
-SEMAPHORES = (["ld", "loc", "st", "c1", "c2", "idd", "pn"]
+SEMAPHORES = (["ld", "loc", "st", "c1", "c2", "idd", "pn", "dgd", "pbd", "ud"]
               + ["%s%d" % (n, i) for n in ("arr", "sqd", "srt", "rec") for i in range(N)]
               + ["%s%d" % (n, i) for n in ("pe", "qsc", "tr", "fin") for i in range(N - 1)])
 
@@ -55,6 +58,7 @@ def rank_program(g, core, T, topo):
     if r is None:
         return
     A = ActivationFunctionType
+    MUL = AluOpType.mult
     sem = T.sem
 
     def blk(t, s):
@@ -75,20 +79,25 @@ def rank_program(g, core, T, topo):
     src = [rd.index(r) for rd in rounds]
 
     g.sync.dma_start(blk(T.land, r), T.x[:]).then_inc(sem.ld, 16)
-    g.vector.memset(T.ones[:], 1.0).then_inc(sem.c1, 1)
     g.vector.memset(T.ident[:], 1.0).then_inc(sem.c2, 1)
-
-    ids = []
-    for p in peers:
-        rid, pid = topo.addr(T.cores[p], core)
-        ids.append(DstId(rid=rid, pnc=pid))
-    g.wait_ge(sem.ld, 16)
-    g.remote_dma_fused([RemoteDMATransfer(dst_ids=ids, dma_engine_mask=engines(r), remote_sem=sem["arr%d" % r],
-                                          srcs=[blk(T.land, r)], dsts=[blk(T.land, r)] * len(ids), alu_op=0)],
-                       local_sem=sem.loc)
+    g.vector.memset(T.ones[:], 1.0).then_inc(sem.c1, 1)
     g.wait_ge(sem.c2, 1)
     g.affine_select(T.ident[:], T.ident[:], [[-1, C]], AluOpType.is_equal, 0.0, 0, 1).then_inc(sem.idd, 1)
-    g.wait_ge(sem.loc, bin(engines(r)).count("1"))
+
+    def send(to, src_ap):
+        ids = []
+        for p in to:
+            rid, pid = topo.addr(T.cores[p], core)
+            ids.append(DstId(rid=rid, pnc=pid))
+        g.remote_dma_fused([RemoteDMATransfer(dst_ids=ids, dma_engine_mask=engines(r), remote_sem=sem["arr%d" % r],
+                                              srcs=[src_ap], dsts=[blk(T.land, r)] * len(ids), alu_op=0)],
+                           local_sem=sem.loc)
+
+    g.wait_ge(sem.ld, 16)
+    send(peers[:RAW], blk(T.land, r))
+    g.wait_ge(sem.ud, 1)
+    send(peers[RAW:], T.u[:])
+    g.wait_ge(sem.loc, 2 * bin(engines(r)).count("1"))
 
     g.scalar.wait_ge(sem.ld, 16)
     g.scalar.activation(blk(T.sq, r), blk(T.land, r), A.Square).then_inc(sem["sqd%d" % r], 1)
@@ -100,10 +109,17 @@ def rank_program(g, core, T, topo):
     g.scalar.activation(col(T.ln, r), T.pown[:, 0:1], A.Sqrt, bias=TINY).then_inc(sem["srt%d" % r], 1)
     g.vector.wait_ge(sem["srt%d" % r], 1)
     g.vector.reciprocal(col(T.inv, r), col(T.ln, r)).then_inc(sem["rec%d" % r], 1)
+    g.vector.wait_ge(sem["rec%d" % r], 1)
+    g.vector.wait_ge(sem.idd, 1)
+    g.vector.tensor_scalar(T.dg[:], T.ident[:], col(T.inv, r), None, MUL).then_inc(sem.dgd, 1)
+    g.tensor.wait_ge(sem.dgd, 1)
+    g.tensor.matmul(T.pown[:, C:2 * C], T.ones[:], T.dg[:], True, True).then_inc(sem.pbd, 1)
+    g.vector.wait_ge(sem.pbd, 1)
+    g.vector.wait_ge(sem.ld, 16)
+    g.vector.tensor_tensor(T.u[:], blk(T.land, r), T.pown[:, C:2 * C], MUL).then_inc(sem.ud, 1)
 
     pq = [T.pq0, T.pq1, T.pq2, T.pq3, T.pq4]
     pt = [T.pt0, T.pt1]
-    last = N - 2
 
     def turn(k):
         g.tensor.wait_ge(sem["qsc%d" % k], 1)
@@ -112,33 +128,34 @@ def rank_program(g, core, T, topo):
         if k >= 2:
             g.tensor.wait_ge(sem["fin%d" % (k - 2)], 1)
         g.tensor.transpose(pt[k % 2][:, 0:C], blk(T.qs, src[k]), T.ident[:]).then_inc(sem["tr%d" % k], 1)
+        g.scalar.wait_ge(sem["tr%d" % k], 1)
+        g.scalar.wait_ge(sem["rec%d" % r], 1)
+        g.scalar.activation(blk(T.yb, src[k]), pt[k % 2][:, 0:C], A.Copy, scale=col(T.inv, r)).then_inc(sem["fin%d" % k], 1)
 
     for k, s in enumerate(src):
         rs, rn = sem["arr%d" % s], bin(engines(s)).count("1")
         g.tensor.wait_ge(rs, rn)
-        g.tensor.matmul(pq[k][:, 0:C], blk(T.land, s), blk(T.land, r), True, True).then_inc(sem["pe%d" % k], 1)
-        g.scalar.wait_ge(rs, rn)
-        g.scalar.activation(blk(T.sq, s), blk(T.land, s), A.Square).then_inc(sem["sqd%d" % s], 1)
-        g.tensor.wait_ge(sem["sqd%d" % s], 1)
-        g.tensor.matmul(pq[k][:, C:C + 1], blk(T.sq, s), T.ones[:, 0:1], True, True).then_inc(sem["pe%d" % k], 1)
-        g.scalar.wait_ge(sem["pe%d" % k], 2)
-        g.scalar.activation(col(T.ln, s), pq[k][:, C:C + 1], A.Sqrt, bias=TINY).then_inc(sem["srt%d" % s], 1)
-        g.vector.wait_ge(sem["srt%d" % s], 1)
-        g.vector.reciprocal(col(T.inv, s), col(T.ln, s)).then_inc(sem["rec%d" % s], 1)
-        g.vector.wait_ge(sem["rec%d" % s], 1)
-        g.vector.wait_ge(sem["pe%d" % k], 2)
-        g.vector.tensor_scalar(blk(T.qs, s), pq[k][:, 0:C], col(T.inv, s), None, AluOpType.mult).then_inc(sem["qsc%d" % k], 1)
-        if k >= 1:
-            turn(k - 1)
-            g.scalar.wait_ge(sem["tr%d" % (k - 1)], 1)
-            g.scalar.wait_ge(sem["rec%d" % r], 1)
-            g.scalar.activation(blk(T.yb, src[k - 1]), pt[(k - 1) % 2][:, 0:C], A.Copy,
-                                scale=col(T.inv, r)).then_inc(sem["fin%d" % (k - 1)], 1)
-    turn(last)
-    g.vector.wait_ge(sem["tr%d" % last], 1)
-    g.vector.wait_ge(sem["rec%d" % r], 1)
-    g.vector.tensor_scalar(blk(T.yb, src[last]), pt[last % 2][:, 0:C], col(T.inv, r), None,
-                           AluOpType.mult).then_inc(sem["fin%d" % last], 1)
+        if k < RAW:
+            g.tensor.matmul(pq[k][:, 0:C], blk(T.land, s), blk(T.land, r), True, True).then_inc(sem["pe%d" % k], 1)
+            g.scalar.wait_ge(rs, rn)
+            g.scalar.activation(blk(T.sq, s), blk(T.land, s), A.Square).then_inc(sem["sqd%d" % s], 1)
+            g.tensor.wait_ge(sem["sqd%d" % s], 1)
+            g.tensor.matmul(pq[k][:, C:C + 1], blk(T.sq, s), T.ones[:, 0:1], True, True).then_inc(sem["pe%d" % k], 1)
+            g.scalar.wait_ge(sem["pe%d" % k], 2)
+            g.scalar.activation(col(T.ln, s), pq[k][:, C:C + 1], A.Sqrt, bias=TINY).then_inc(sem["srt%d" % s], 1)
+            g.vector.wait_ge(sem["srt%d" % s], 1)
+            g.vector.reciprocal(col(T.inv, s), col(T.ln, s)).then_inc(sem["rec%d" % s], 1)
+            g.vector.wait_ge(sem["rec%d" % s], 1)
+            g.vector.wait_ge(sem["pe%d" % k], 2)
+            g.vector.tensor_scalar(blk(T.qs, s), pq[k][:, 0:C], col(T.inv, s), None, MUL).then_inc(sem["qsc%d" % k], 1)
+            if k >= 1:
+                turn(k - 1)
+            if k == RAW - 1:
+                turn(k)
+        else:
+            g.tensor.matmul(pq[k][:, 0:C], blk(T.land, r), blk(T.land, s), True, True).then_inc(sem["pe%d" % k], 1)
+            g.vector.wait_ge(sem["pe%d" % k], 1)
+            g.vector.tensor_scalar(blk(T.yb, s), pq[k][:, 0:C], col(T.inv, r), None, MUL).then_inc(sem["fin%d" % k], 1)
 
     for k, s in enumerate(src):
         g.sync.wait_ge(sem["fin%d" % k], 1)

@@ -3,7 +3,7 @@ from concourse.mybir import AluOpType, ActivationFunctionType
 
 N = 6
 C = 128
-RAW = 3
+RAW = 2
 TINY = 2e-35
 
 SCRATCH = {

@@ -3,19 +3,21 @@ from concourse.mybir import AluOpType, ActivationFunctionType
 
 N = 6
 C = 128
-RAW = 2
+RAW = 3
 TINY = 2e-35
 
 SCRATCH = {
     "land": ("sbuf", [128, N * C], "bfloat16"),
     "sq": ("sbuf", [128, N * C], "bfloat16"),
-    "qs": ("sbuf", [128, N * C], "bfloat16"),
+    "qs": ("sbuf", [128, RAW * C], "bfloat16"),
+    "dgs": ("sbuf", [128, RAW * C], "bfloat16"),
     "yb": ("sbuf", [128, N * C], "bfloat16"),
     "ones": ("sbuf", [128, C], "bfloat16"),
+    "tiny": ("sbuf", [128, 8], "bfloat16"),
     "ident": ("sbuf", [128, C], "bfloat16"),
     "dg": ("sbuf", [128, C], "bfloat16"),
     "u": ("sbuf", [128, C], "bfloat16"),
-    "ln": ("sbuf", [128, 8], "float32"),
+    "rss": ("sbuf", [128, 8], "float32"),
     "inv": ("sbuf", [128, 8], "float32"),
     "pq0": ("psum", [128, 512], "float32"),
     "pq1": ("psum", [128, 512], "float32"),
@@ -23,12 +25,12 @@ SCRATCH = {
     "pq3": ("psum", [128, 512], "float32"),
     "pq4": ("psum", [128, 512], "float32"),
     "pown": ("psum", [128, 512], "float32"),
-    "pt0": ("psum", [128, 1024], "bfloat16"),
-    "pt1": ("psum", [128, 1024], "bfloat16"),
+    "pss": ("psum", [128, 512], "float32"),
 }
-SEMAPHORES = (["ld", "loc", "st", "c1", "c2", "idd", "pn", "dgd", "pbd", "ud"]
-              + ["%s%d" % (n, i) for n in ("arr", "sqd", "srt", "rec") for i in range(N)]
-              + ["%s%d" % (n, i) for n in ("pe", "qsc", "tr", "fin") for i in range(N - 1)])
+SEMAPHORES = (["ld", "loc", "st", "st2", "c1", "c2", "c3", "idd", "sqo", "pn", "rro", "dgd", "invd", "pbd", "ud",
+               "pns", "rrd"]
+              + ["arr%d" % i for i in range(N)]
+              + ["%s%d" % (n, i) for n in ("sqd", "pe", "qc", "dd", "tr", "fin") for i in range(N - 1)])
 
 
 def plan(near):
@@ -60,12 +62,10 @@ def rank_program(g, core, T, topo):
     A = ActivationFunctionType
     MUL = AluOpType.mult
     sem = T.sem
+    pe, act, dve = g.tensor, g.scalar, g.vector
 
     def blk(t, s):
         return t[:, s * C:(s + 1) * C]
-
-    def col(t, s):
-        return t[:, s:s + 1]
 
     def engines(s):
         m = -1
@@ -74,13 +74,24 @@ def rank_program(g, core, T, topo):
                 m &= topo.mask(T.cores[s], d)
         return m
 
+    def landed(q, s):
+        q.wait_ge(sem["arr%d" % s], bin(engines(s)).count("1"))
+
+    def sumsq(out, s):
+        pe.matmul(out, blk(T.sq, s), T.ones[:, 0:1], True, False)
+        return pe.matmul(out, T.ones[0:1, :], T.tiny[0:1, 0:1], False, True)
+
     rounds = plan([[a != b and topo.same_plane(T.cores[a], T.cores[b]) for b in range(N)] for a in range(N)])
     peers = [rd[r] for rd in rounds]
     src = [rd.index(r) for rd in rounds]
+    xr = blk(T.land, r)
+    rso = T.rss[:, 7:8]
+    inv = T.inv[:, 0:1]
 
-    g.sync.dma_start(blk(T.land, r), T.x[:]).then_inc(sem.ld, 16)
-    g.vector.memset(T.ident[:], 1.0).then_inc(sem.c2, 1)
-    g.vector.memset(T.ones[:], 1.0).then_inc(sem.c1, 1)
+    g.sync.dma_start(xr, T.x[:]).then_inc(sem.ld, 16)
+    dve.memset(T.ident[:], 1.0).then_inc(sem.c2, 1)
+    dve.memset(T.ones[:], 1.0).then_inc(sem.c1, 1)
+    dve.memset(T.tiny[:], TINY).then_inc(sem.c3, 1)
     g.wait_ge(sem.c2, 1)
     g.affine_select(T.ident[:], T.ident[:], [[-1, C]], AluOpType.is_equal, 0.0, 0, 1).then_inc(sem.idd, 1)
 
@@ -90,74 +101,69 @@ def rank_program(g, core, T, topo):
             rid, pid = topo.addr(T.cores[p], core)
             ids.append(DstId(rid=rid, pnc=pid))
         g.remote_dma_fused([RemoteDMATransfer(dst_ids=ids, dma_engine_mask=engines(r), remote_sem=sem["arr%d" % r],
-                                              srcs=[src_ap], dsts=[blk(T.land, r)] * len(ids), alu_op=0)],
-                           local_sem=sem.loc)
+                                              srcs=[src_ap], dsts=[xr] * len(ids), alu_op=0)], local_sem=sem.loc)
 
     g.wait_ge(sem.ld, 16)
-    send(peers[:RAW], blk(T.land, r))
+    send(peers[:RAW], xr)
     g.wait_ge(sem.ud, 1)
     send(peers[RAW:], T.u[:])
     g.wait_ge(sem.loc, 2 * bin(engines(r)).count("1"))
 
-    g.scalar.wait_ge(sem.ld, 16)
-    g.scalar.activation(blk(T.sq, r), blk(T.land, r), A.Square).then_inc(sem["sqd%d" % r], 1)
-    g.tensor.wait_ge(sem["sqd%d" % r], 1)
-    g.tensor.wait_ge(sem.c1, 1)
-    g.tensor.wait_ge(sem.ld, 16)
-    g.tensor.matmul(T.pown[:, 0:1], blk(T.sq, r), T.ones[:, 0:1], True, True).then_inc(sem.pn, 1)
-    g.scalar.wait_ge(sem.pn, 1)
-    g.scalar.activation(col(T.ln, r), T.pown[:, 0:1], A.Sqrt, bias=TINY).then_inc(sem["srt%d" % r], 1)
-    g.vector.wait_ge(sem["srt%d" % r], 1)
-    g.vector.reciprocal(col(T.inv, r), col(T.ln, r)).then_inc(sem["rec%d" % r], 1)
-    g.vector.wait_ge(sem["rec%d" % r], 1)
-    g.vector.wait_ge(sem.idd, 1)
-    g.vector.tensor_scalar(T.dg[:], T.ident[:], col(T.inv, r), None, MUL).then_inc(sem.dgd, 1)
-    g.tensor.wait_ge(sem.dgd, 1)
-    g.tensor.matmul(T.pown[:, C:2 * C], T.ones[:], T.dg[:], True, True).then_inc(sem.pbd, 1)
-    g.vector.wait_ge(sem.pbd, 1)
-    g.vector.wait_ge(sem.ld, 16)
-    g.vector.tensor_tensor(T.u[:], blk(T.land, r), T.pown[:, C:2 * C], MUL).then_inc(sem.ud, 1)
+    act.wait_ge(sem.ld, 16)
+    act.activation(blk(T.sq, r), xr, A.Square).then_inc(sem.sqo, 1)
+    pe.wait_ge(sem.sqo, 1)
+    pe.wait_ge(sem.c1, 1)
+    pe.wait_ge(sem.c3, 1)
+    pe.wait_ge(sem.ld, 16)
+    sumsq(T.pown[:, 0:1], r).then_inc(sem.pn, 1)
+    dve.wait_ge(sem.pn, 1)
+    dve.reciprocal(rso, T.pown[:, 0:1]).then_inc(sem.rro, 1)
+    act.wait_ge(sem.rro, 1)
+    act.wait_ge(sem.idd, 1)
+    act.activation(T.dg[:], T.ident[:], A.Sqrt, scale=rso).then_inc(sem.dgd, 1)
+    act.activation(inv, rso, A.Sqrt).then_inc(sem.invd, 1)
+    pe.wait_ge(sem.dgd, 1)
+    pe.matmul(T.pown[:, C:2 * C], T.ones[:], T.dg[:], True, True).then_inc(sem.pbd, 1)
+    dve.wait_ge(sem.pbd, 1)
+    dve.wait_ge(sem.ld, 16)
+    dve.tensor_tensor(T.u[:], xr, T.pown[:, C:2 * C], MUL).then_inc(sem.ud, 1)
 
     pq = [T.pq0, T.pq1, T.pq2, T.pq3, T.pq4]
-    pt = [T.pt0, T.pt1]
+    raw = list(range(RAW))
+    for k in raw:
+        landed(pe, src[k])
+        pe.matmul(pq[k][:, 0:C], blk(T.land, src[k]), xr, True, True).then_inc(sem["pe%d" % k], 1)
+        landed(act, src[k])
+        act.activation(blk(T.sq, src[k]), blk(T.land, src[k]), A.Square).then_inc(sem["sqd%d" % k], 1)
+    for k in raw:
+        pe.wait_ge(sem["sqd%d" % k], 1)
+        sumsq(T.pss[:, k:k + 1], src[k]).then_inc(sem.pns, 1)
+    dve.wait_ge(sem.pns, RAW)
+    dve.reciprocal(T.rss[:, 0:RAW], T.pss[:, 0:RAW]).then_inc(sem.rrd, 1)
+    act.wait_ge(sem.rrd, 1)
+    for k in raw:
+        act.activation(blk(T.dgs, k), T.ident[:], A.Sqrt, scale=T.rss[:, k:k + 1]).then_inc(sem["dd%d" % k], 1)
+        dve.wait_ge(sem["pe%d" % k], 1)
+        dve.tensor_copy(blk(T.qs, k), pq[k][:, 0:C]).then_inc(sem["qc%d" % k], 1)
+    act.wait_ge(sem.invd, 1)
+    for k in raw:
+        pe.wait_ge(sem["dd%d" % k], 1)
+        pe.wait_ge(sem["qc%d" % k], 1)
+        pe.matmul(pq[k][:, C:2 * C], blk(T.qs, k), blk(T.dgs, k), True, True).then_inc(sem["tr%d" % k], 1)
+        act.wait_ge(sem["tr%d" % k], 1)
+        act.activation(blk(T.yb, src[k]), pq[k][:, C:2 * C], A.Copy, scale=inv).then_inc(sem["fin%d" % k], 1)
+    for k in raw:
+        act.wait_ge(sem["fin%d" % k], 1)
+        act.dma_start(blk(T.y, src[k]), blk(T.yb, src[k])).then_inc(sem.st2, 16)
 
-    def turn(k):
-        g.tensor.wait_ge(sem["qsc%d" % k], 1)
-        if k == 0:
-            g.tensor.wait_ge(sem.idd, 1)
-        if k >= 2:
-            g.tensor.wait_ge(sem["fin%d" % (k - 2)], 1)
-        g.tensor.transpose(pt[k % 2][:, 0:C], blk(T.qs, src[k]), T.ident[:]).then_inc(sem["tr%d" % k], 1)
-        g.scalar.wait_ge(sem["tr%d" % k], 1)
-        g.scalar.wait_ge(sem["rec%d" % r], 1)
-        g.scalar.activation(blk(T.yb, src[k]), pt[k % 2][:, 0:C], A.Copy, scale=col(T.inv, r)).then_inc(sem["fin%d" % k], 1)
-
-    for k, s in enumerate(src):
-        rs, rn = sem["arr%d" % s], bin(engines(s)).count("1")
-        g.tensor.wait_ge(rs, rn)
-        if k < RAW:
-            g.tensor.matmul(pq[k][:, 0:C], blk(T.land, s), blk(T.land, r), True, True).then_inc(sem["pe%d" % k], 1)
-            g.scalar.wait_ge(rs, rn)
-            g.scalar.activation(blk(T.sq, s), blk(T.land, s), A.Square).then_inc(sem["sqd%d" % s], 1)
-            g.tensor.wait_ge(sem["sqd%d" % s], 1)
-            g.tensor.matmul(pq[k][:, C:C + 1], blk(T.sq, s), T.ones[:, 0:1], True, True).then_inc(sem["pe%d" % k], 1)
-            g.scalar.wait_ge(sem["pe%d" % k], 2)
-            g.scalar.activation(col(T.ln, s), pq[k][:, C:C + 1], A.Sqrt, bias=TINY).then_inc(sem["srt%d" % s], 1)
-            g.vector.wait_ge(sem["srt%d" % s], 1)
-            g.vector.reciprocal(col(T.inv, s), col(T.ln, s)).then_inc(sem["rec%d" % s], 1)
-            g.vector.wait_ge(sem["rec%d" % s], 1)
-            g.vector.wait_ge(sem["pe%d" % k], 2)
-            g.vector.tensor_scalar(blk(T.qs, s), pq[k][:, 0:C], col(T.inv, s), None, MUL).then_inc(sem["qsc%d" % k], 1)
-            if k >= 1:
-                turn(k - 1)
-            if k == RAW - 1:
-                turn(k)
-        else:
-            g.tensor.matmul(pq[k][:, 0:C], blk(T.land, r), blk(T.land, s), True, True).then_inc(sem["pe%d" % k], 1)
-            g.vector.wait_ge(sem["pe%d" % k], 1)
-            g.vector.tensor_scalar(blk(T.yb, s), pq[k][:, 0:C], col(T.inv, r), None, MUL).then_inc(sem["fin%d" % k], 1)
-
-    for k, s in enumerate(src):
+    dve.wait_ge(sem.invd, 1)
+    for k in range(RAW, N - 1):
+        s = src[k]
+        landed(pe, s)
+        pe.matmul(pq[k][:, 0:C], xr, blk(T.land, s), True, True).then_inc(sem["pe%d" % k], 1)
+        dve.wait_ge(sem["pe%d" % k], 1)
+        dve.tensor_scalar(blk(T.yb, s), pq[k][:, 0:C], inv, None, MUL).then_inc(sem["fin%d" % k], 1)
         g.sync.wait_ge(sem["fin%d" % k], 1)
         g.sync.dma_start(blk(T.y, s), blk(T.yb, s)).then_inc(sem.st, 16)
-    g.sync.wait_ge(sem.st, 16 * (N - 1))
+    g.sync.wait_ge(sem.st, 16 * (N - 1 - RAW))
+    act.wait_ge(sem.st2, 16 * RAW)

@@ -3,7 +3,7 @@ from concourse.mybir import AluOpType, ActivationFunctionType
 
 N = 6
 C = 128
-RAW = 3
+RAW = 2
 TINY = 2e-35
 
 SCRATCH = {
@@ -12,6 +12,7 @@ SCRATCH = {
     "qs": ("sbuf", [128, RAW * C], "bfloat16"),
     "dgs": ("sbuf", [128, RAW * C], "bfloat16"),
     "yb": ("sbuf", [128, N * C], "bfloat16"),
+    "base": ("sbuf", [128, C], "bfloat16"),
     "ones": ("sbuf", [128, C], "bfloat16"),
     "tiny": ("sbuf", [128, 8], "bfloat16"),
     "ident": ("sbuf", [128, C], "bfloat16"),
@@ -78,8 +79,8 @@ def rank_program(g, core, T, topo):
         q.wait_ge(sem["arr%d" % s], bin(engines(s)).count("1"))
 
     def sumsq(out, s):
-        pe.matmul(out, blk(T.sq, s), T.ones[:, 0:1], True, False)
-        return pe.matmul(out, T.ones[0:1, :], T.tiny[0:1, 0:1], False, True)
+        pe.matmul(out, blk(T.sq, s), T.base[:, 0:1], True, False)
+        return pe.matmul(out, T.base[0:1, :], T.tiny[0:1, 0:1], False, True)
 
     rounds = plan([[a != b and topo.same_plane(T.cores[a], T.cores[b]) for b in range(N)] for a in range(N)])
     peers = [rd[r] for rd in rounds]
@@ -89,11 +90,12 @@ def rank_program(g, core, T, topo):
     inv = T.inv[:, 0:1]
 
     g.sync.dma_start(xr, T.x[:]).then_inc(sem.ld, 16)
-    dve.memset(T.ident[:], 1.0).then_inc(sem.c2, 1)
-    dve.memset(T.ones[:], 1.0).then_inc(sem.c1, 1)
+    dve.memset(T.base[:], 1.0).then_inc(sem.c2, 1)
     dve.memset(T.tiny[:], TINY).then_inc(sem.c3, 1)
+    act.wait_ge(sem.c2, 1)
+    act.activation(T.ones[:], T.base[:], A.Sqrt).then_inc(sem.c1, 1)
     g.wait_ge(sem.c2, 1)
-    g.affine_select(T.ident[:], T.ident[:], [[-1, C]], AluOpType.is_equal, 0.0, 0, 1).then_inc(sem.idd, 1)
+    g.affine_select(T.ident[:], T.base[:], [[-1, C]], AluOpType.is_equal, 0.0, 0, 1).then_inc(sem.idd, 1)
 
     def send(to, src_ap):
         ids = []
@@ -109,10 +111,10 @@ def rank_program(g, core, T, topo):
     send(peers[RAW:], T.u[:])
     g.wait_ge(sem.loc, 2 * bin(engines(r)).count("1"))
 
-    act.wait_ge(sem.ld, 16)
-    act.activation(blk(T.sq, r), xr, A.Square).then_inc(sem.sqo, 1)
+    dve.wait_ge(sem.ld, 16)
+    dve.tensor_tensor(blk(T.sq, r), xr, xr, MUL).then_inc(sem.sqo, 1)
     pe.wait_ge(sem.sqo, 1)
-    pe.wait_ge(sem.c1, 1)
+    pe.wait_ge(sem.c2, 1)
     pe.wait_ge(sem.c3, 1)
     pe.wait_ge(sem.ld, 16)
     sumsq(T.pown[:, 0:1], r).then_inc(sem.pn, 1)
@@ -123,9 +125,9 @@ def rank_program(g, core, T, topo):
     act.activation(T.dg[:], T.ident[:], A.Sqrt, scale=rso).then_inc(sem.dgd, 1)
     act.activation(inv, rso, A.Sqrt).then_inc(sem.invd, 1)
     pe.wait_ge(sem.dgd, 1)
+    pe.wait_ge(sem.c1, 1)
     pe.matmul(T.pown[:, C:2 * C], T.ones[:], T.dg[:], True, True).then_inc(sem.pbd, 1)
     dve.wait_ge(sem.pbd, 1)
-    dve.wait_ge(sem.ld, 16)
     dve.tensor_tensor(T.u[:], xr, T.pown[:, C:2 * C], MUL).then_inc(sem.ud, 1)
 
     pq = [T.pq0, T.pq1, T.pq2, T.pq3, T.pq4]

@@ -18,7 +18,7 @@ SCRATCH = {
     "ident": ("sbuf", [128, C], "bfloat16"),
     "dg": ("sbuf", [128, C], "bfloat16"),
     "u": ("sbuf", [128, C], "bfloat16"),
-    "rss": ("sbuf", [128, 8], "float32"),
+    "rss": ("sbuf", [128, 12], "float32"),
     "inv": ("sbuf", [128, 8], "float32"),
     "pq0": ("psum", [128, 512], "float32"),
     "pq1": ("psum", [128, 512], "float32"),
@@ -26,12 +26,12 @@ SCRATCH = {
     "pq3": ("psum", [128, 512], "float32"),
     "pq4": ("psum", [128, 512], "float32"),
     "pown": ("psum", [128, 512], "float32"),
-    "pss": ("psum", [128, 512], "float32"),
+    "pss0": ("psum", [128, 512], "float32"),
+    "pss1": ("psum", [128, 512], "float32"),
 }
-SEMAPHORES = (["ld", "loc", "st", "st2", "c1", "c2", "c3", "idd", "sqo", "pn", "rro", "dgd", "invd", "pbd", "ud",
-               "pns", "rrd"]
+SEMAPHORES = (["ld", "loc", "st", "st2", "c1", "c2", "c3", "idd", "sqo", "pn", "rro", "dgd", "invd", "pbd", "ud"]
               + ["arr%d" % i for i in range(N)]
-              + ["%s%d" % (n, i) for n in ("sqd", "pe", "qc", "dd", "tr", "fin") for i in range(N - 1)])
+              + ["%s%d" % (n, i) for n in ("sqd", "pns", "rrd", "pe", "qc", "dd", "tr", "fin") for i in range(N - 1)])
 
 
 def plan(near):
@@ -78,16 +78,15 @@ def rank_program(g, core, T, topo):
     def landed(q, s):
         q.wait_ge(sem["arr%d" % s], bin(engines(s)).count("1"))
 
-    def sumsq(out, s):
-        pe.matmul(out, blk(T.sq, s), T.base[:, 0:1], True, False)
-        return pe.matmul(out, T.base[0:1, :], T.tiny[0:1, 0:1], False, True)
-
     rounds = plan([[a != b and topo.same_plane(T.cores[a], T.cores[b]) for b in range(N)] for a in range(N)])
     peers = [rd[r] for rd in rounds]
     src = [rd.index(r) for rd in rounds]
     xr = blk(T.land, r)
-    rso = T.rss[:, 7:8]
+    rso = T.rss[:, 8:9]
     inv = T.inv[:, 0:1]
+    pq = [T.pq0, T.pq1, T.pq2, T.pq3, T.pq4]
+    pss = [T.pss0, T.pss1]
+    raw = list(range(RAW))
 
     g.sync.dma_start(xr, T.x[:]).then_inc(sem.ld, 16)
     dve.memset(T.base[:], 1.0).then_inc(sem.c2, 1)
@@ -113,11 +112,12 @@ def rank_program(g, core, T, topo):
 
     dve.wait_ge(sem.ld, 16)
     dve.tensor_tensor(blk(T.sq, r), xr, xr, MUL).then_inc(sem.sqo, 1)
-    pe.wait_ge(sem.sqo, 1)
     pe.wait_ge(sem.c2, 1)
     pe.wait_ge(sem.c3, 1)
-    pe.wait_ge(sem.ld, 16)
-    sumsq(T.pown[:, 0:1], r).then_inc(sem.pn, 1)
+    for out in [T.pown] + pss:
+        pe.matmul(out[:, 0:1], T.base[0:1, :], T.tiny[0:1, 0:1], True, False)
+    pe.wait_ge(sem.sqo, 1)
+    pe.matmul(T.pown[:, 0:1], blk(T.sq, r), T.base[:, 0:1], False, True).then_inc(sem.pn, 1)
     dve.wait_ge(sem.pn, 1)
     dve.reciprocal(rso, T.pown[:, 0:1]).then_inc(sem.rro, 1)
     act.wait_ge(sem.rro, 1)
@@ -130,36 +130,25 @@ def rank_program(g, core, T, topo):
     dve.wait_ge(sem.pbd, 1)
     dve.tensor_tensor(T.u[:], xr, T.pown[:, C:2 * C], MUL).then_inc(sem.ud, 1)
 
-    pq = [T.pq0, T.pq1, T.pq2, T.pq3, T.pq4]
-    raw = list(range(RAW))
+    pe.wait_ge(sem.ld, 16)
     for k in raw:
-        landed(pe, src[k])
-        pe.matmul(pq[k][:, 0:C], blk(T.land, src[k]), xr, True, True).then_inc(sem["pe%d" % k], 1)
-        landed(act, src[k])
-        act.activation(blk(T.sq, src[k]), blk(T.land, src[k]), A.Square).then_inc(sem["sqd%d" % k], 1)
-    for k in raw:
+        s = src[k]
+        landed(pe, s)
+        pe.matmul(pq[k][:, 0:C], blk(T.land, s), xr, True, True).then_inc(sem["pe%d" % k], 1)
+        landed(act, s)
+        act.activation(blk(T.sq, s), blk(T.land, s), A.Square).then_inc(sem["sqd%d" % k], 1)
         pe.wait_ge(sem["sqd%d" % k], 1)
-        sumsq(T.pss[:, k:k + 1], src[k]).then_inc(sem.pns, 1)
-    dve.wait_ge(sem.pns, RAW)
-    dve.reciprocal(T.rss[:, 0:RAW], T.pss[:, 0:RAW]).then_inc(sem.rrd, 1)
-    act.wait_ge(sem.rrd, 1)
-    for k in raw:
-        act.activation(blk(T.dgs, k), T.ident[:], A.Sqrt, scale=T.rss[:, k:k + 1]).then_inc(sem["dd%d" % k], 1)
+        pe.matmul(pss[k][:, 0:1], blk(T.sq, s), T.base[:, 0:1], False, True).then_inc(sem["pns%d" % k], 1)
         dve.wait_ge(sem["pe%d" % k], 1)
         dve.tensor_copy(blk(T.qs, k), pq[k][:, 0:C]).then_inc(sem["qc%d" % k], 1)
-    act.wait_ge(sem.invd, 1)
+        dve.wait_ge(sem["pns%d" % k], 1)
+        dve.reciprocal(T.rss[:, 4 * k:4 * k + 1], pss[k][:, 0:1]).then_inc(sem["rrd%d" % k], 1)
     for k in raw:
-        pe.wait_ge(sem["dd%d" % k], 1)
-        pe.wait_ge(sem["qc%d" % k], 1)
-        pe.matmul(pq[k][:, C:2 * C], blk(T.qs, k), blk(T.dgs, k), True, True).then_inc(sem["tr%d" % k], 1)
-        act.wait_ge(sem["tr%d" % k], 1)
-        act.activation(blk(T.yb, src[k]), pq[k][:, C:2 * C], A.Copy, scale=inv).then_inc(sem["fin%d" % k], 1)
-    for k in raw:
-        act.wait_ge(sem["fin%d" % k], 1)
-        act.dma_start(blk(T.y, src[k]), blk(T.yb, src[k])).then_inc(sem.st2, 16)
+        act.wait_ge(sem["rrd%d" % k], 1)
+        act.activation(blk(T.dgs, k), T.ident[:], A.Sqrt,
+                       scale=T.rss[:, 4 * k:4 * k + 1]).then_inc(sem["dd%d" % k], 1)
 
-    dve.wait_ge(sem.invd, 1)
-    for k in range(RAW, N - 1):
+    def ublock(k):
         s = src[k]
         landed(pe, s)
         pe.matmul(pq[k][:, 0:C], xr, blk(T.land, s), True, True).then_inc(sem["pe%d" % k], 1)
@@ -167,5 +156,23 @@ def rank_program(g, core, T, topo):
         dve.tensor_scalar(blk(T.yb, s), pq[k][:, 0:C], inv, None, MUL).then_inc(sem["fin%d" % k], 1)
         g.sync.wait_ge(sem["fin%d" % k], 1)
         g.sync.dma_start(blk(T.y, s), blk(T.yb, s)).then_inc(sem.st, 16)
-    g.sync.wait_ge(sem.st, 16 * (N - 1 - RAW))
-    act.wait_ge(sem.st2, 16 * RAW)
+
+    dve.wait_ge(sem.invd, 1)
+    for k in range(RAW, N - 2):
+        ublock(k)
+
+    act.wait_ge(sem.invd, 1)
+    for k in raw:
+        pe.wait_ge(sem["dd%d" % k], 1)
+        pe.wait_ge(sem["qc%d" % k], 1)
+        pe.matmul(pq[k][:, C:2 * C], blk(T.qs, k), blk(T.dgs, k), True, True).then_inc(sem["tr%d" % k], 1)
+        act.wait_ge(sem["tr%d" % k], 1)
+        act.activation(blk(T.yb, src[k]), pq[k][:, C:2 * C], A.Copy, scale=inv).then_inc(sem["fin%d" % k], 1)
+    g.sync.wait_ge(sem.fin0, 1)
+    g.sync.dma_start(blk(T.y, src[0]), blk(T.yb, src[0])).then_inc(sem.st, 16)
+    act.wait_ge(sem.fin1, 1)
+    act.dma_start(blk(T.y, src[1]), blk(T.yb, src[1])).then_inc(sem.st2, 16)
+
+    ublock(N - 2)
+    g.sync.wait_ge(sem.st, 16 * (N - 2))
+    act.wait_ge(sem.st2, 16)

from concourse.bass import DstId, RemoteDMATransfer
from concourse.mybir import AluOpType, ActivationFunctionType

N = 6
C = 128
RAW = 2
TINY = 2e-35

SCRATCH = {
    "land": ("sbuf", [128, N * C], "bfloat16"),
    "sq": ("sbuf", [128, N * C], "bfloat16"),
    "qs": ("sbuf", [128, RAW * C], "bfloat16"),
    "dgs": ("sbuf", [128, RAW * C], "bfloat16"),
    "yb": ("sbuf", [128, N * C], "bfloat16"),
    "base": ("sbuf", [128, C], "bfloat16"),
    "ones": ("sbuf", [128, C], "bfloat16"),
    "tiny": ("sbuf", [128, 8], "bfloat16"),
    "ident": ("sbuf", [128, C], "bfloat16"),
    "dg": ("sbuf", [128, C], "bfloat16"),
    "u": ("sbuf", [128, C], "bfloat16"),
    "rss": ("sbuf", [128, 12], "float32"),
    "inv": ("sbuf", [128, 8], "float32"),
    "pq0": ("psum", [128, 512], "float32"),
    "pq1": ("psum", [128, 512], "float32"),
    "pq2": ("psum", [128, 512], "float32"),
    "pq3": ("psum", [128, 512], "float32"),
    "pq4": ("psum", [128, 512], "float32"),
    "pown": ("psum", [128, 512], "float32"),
    "pss0": ("psum", [128, 512], "float32"),
    "pss1": ("psum", [128, 512], "float32"),
}
SEMAPHORES = (["ld", "loc", "st", "st2", "c1", "c2", "c3", "idd", "sqo", "pn", "rro", "dgd", "invd", "pbd", "ud"]
              + ["arr%d" % i for i in range(N)]
              + ["%s%d" % (n, i) for n in ("sqd", "pns", "rrd", "pe", "qc", "dd", "tr", "fin") for i in range(N - 1)])


def plan(near):
    used = [[a == b for b in range(N)] for a in range(N)]
    rounds = []
    for _ in range(N - 1):
        best = [None, -1]

        def rec(a, perm, score):
            if a == N:
                if score > best[1]:
                    best[0], best[1] = perm, score
                return
            for b in range(N):
                if not used[a][b] and b not in perm:
                    rec(a + 1, perm + [b], score + (1 if near[a][b] else 0))

        rec(0, [], 0)
        for a, b in enumerate(best[0]):
            used[a][b] = True
        rounds.insert(0, best[0])
    return rounds


def rank_program(g, core, T, topo):
    r = T.rank_of(core)
    if r is None:
        return
    A = ActivationFunctionType
    MUL = AluOpType.mult
    sem = T.sem
    pe, act, dve = g.tensor, g.scalar, g.vector

    def blk(t, s):
        return t[:, s * C:(s + 1) * C]

    def engines(s):
        m = -1
        for d in T.cores:
            if d != T.cores[s]:
                m &= topo.mask(T.cores[s], d)
        return m

    def landed(q, s):
        q.wait_ge(sem["arr%d" % s], bin(engines(s)).count("1"))

    rounds = plan([[a != b and topo.same_plane(T.cores[a], T.cores[b]) for b in range(N)] for a in range(N)])
    peers = [rd[r] for rd in rounds]
    src = [rd.index(r) for rd in rounds]
    xr = blk(T.land, r)
    rso = T.rss[:, 8:9]
    inv = T.inv[:, 0:1]
    pq = [T.pq0, T.pq1, T.pq2, T.pq3, T.pq4]
    pss = [T.pss0, T.pss1]
    raw = list(range(RAW))

    g.sync.dma_start(xr, T.x[:]).then_inc(sem.ld, 16)
    dve.memset(T.base[:], 1.0).then_inc(sem.c2, 1)
    dve.memset(T.tiny[:], TINY).then_inc(sem.c3, 1)
    act.wait_ge(sem.c2, 1)
    act.activation(T.ones[:], T.base[:], A.Sqrt).then_inc(sem.c1, 1)
    g.wait_ge(sem.c2, 1)
    g.affine_select(T.ident[:], T.base[:], [[-1, C]], AluOpType.is_equal, 0.0, 0, 1).then_inc(sem.idd, 1)

    def send(to, src_ap):
        ids = []
        for p in to:
            rid, pid = topo.addr(T.cores[p], core)
            ids.append(DstId(rid=rid, pnc=pid))
        g.remote_dma_fused([RemoteDMATransfer(dst_ids=ids, dma_engine_mask=engines(r), remote_sem=sem["arr%d" % r],
                                              srcs=[src_ap], dsts=[xr] * len(ids), alu_op=0)], local_sem=sem.loc)

    g.wait_ge(sem.ld, 16)
    send(peers[:RAW], xr)
    g.wait_ge(sem.ud, 1)
    send(peers[RAW:], T.u[:])
    g.wait_ge(sem.loc, 2 * bin(engines(r)).count("1"))

    dve.wait_ge(sem.ld, 16)
    dve.tensor_tensor(blk(T.sq, r), xr, xr, MUL).then_inc(sem.sqo, 1)
    pe.wait_ge(sem.c2, 1)
    pe.wait_ge(sem.c3, 1)
    for out in [T.pown] + pss:
        pe.matmul(out[:, 0:1], T.base[0:1, :], T.tiny[0:1, 0:1], True, False)
    pe.wait_ge(sem.sqo, 1)
    pe.matmul(T.pown[:, 0:1], blk(T.sq, r), T.base[:, 0:1], False, True).then_inc(sem.pn, 1)
    dve.wait_ge(sem.pn, 1)
    dve.reciprocal(rso, T.pown[:, 0:1]).then_inc(sem.rro, 1)
    act.wait_ge(sem.rro, 1)
    act.wait_ge(sem.idd, 1)
    act.activation(T.dg[:], T.ident[:], A.Sqrt, scale=rso).then_inc(sem.dgd, 1)
    act.activation(inv, rso, A.Sqrt).then_inc(sem.invd, 1)
    pe.wait_ge(sem.dgd, 1)
    pe.wait_ge(sem.c1, 1)
    pe.matmul(T.pown[:, C:2 * C], T.ones[:], T.dg[:], True, True).then_inc(sem.pbd, 1)
    dve.wait_ge(sem.pbd, 1)
    dve.tensor_tensor(T.u[:], xr, T.pown[:, C:2 * C], MUL).then_inc(sem.ud, 1)

    pe.wait_ge(sem.ld, 16)
    for k in raw:
        s = src[k]
        landed(pe, s)
        pe.matmul(pq[k][:, 0:C], blk(T.land, s), xr, True, True).then_inc(sem["pe%d" % k], 1)
        landed(act, s)
        act.activation(blk(T.sq, s), blk(T.land, s), A.Square).then_inc(sem["sqd%d" % k], 1)
        pe.wait_ge(sem["sqd%d" % k], 1)
        pe.matmul(pss[k][:, 0:1], blk(T.sq, s), T.base[:, 0:1], False, True).then_inc(sem["pns%d" % k], 1)
        dve.wait_ge(sem["pe%d" % k], 1)
        dve.tensor_copy(blk(T.qs, k), pq[k][:, 0:C]).then_inc(sem["qc%d" % k], 1)
        dve.wait_ge(sem["pns%d" % k], 1)
        dve.reciprocal(T.rss[:, 4 * k:4 * k + 1], pss[k][:, 0:1]).then_inc(sem["rrd%d" % k], 1)
    for k in raw:
        act.wait_ge(sem["rrd%d" % k], 1)
        act.activation(blk(T.dgs, k), T.ident[:], A.Sqrt,
                       scale=T.rss[:, 4 * k:4 * k + 1]).then_inc(sem["dd%d" % k], 1)

    def ublock(k):
        s = src[k]
        landed(pe, s)
        pe.matmul(pq[k][:, 0:C], xr, blk(T.land, s), True, True).then_inc(sem["pe%d" % k], 1)
        dve.wait_ge(sem["pe%d" % k], 1)
        dve.tensor_scalar(blk(T.yb, s), pq[k][:, 0:C], inv, None, MUL).then_inc(sem["fin%d" % k], 1)
        g.sync.wait_ge(sem["fin%d" % k], 1)
        g.sync.dma_start(blk(T.y, s), blk(T.yb, s)).then_inc(sem.st, 16)

    dve.wait_ge(sem.invd, 1)
    for k in range(RAW, N - 2):
        ublock(k)

    act.wait_ge(sem.invd, 1)
    for k in raw:
        pe.wait_ge(sem["dd%d" % k], 1)
        pe.wait_ge(sem["qc%d" % k], 1)
        pe.matmul(pq[k][:, C:2 * C], blk(T.qs, k), blk(T.dgs, k), True, True).then_inc(sem["tr%d" % k], 1)
        act.wait_ge(sem["tr%d" % k], 1)
        act.activation(blk(T.yb, src[k]), pq[k][:, C:2 * C], A.Copy, scale=inv).then_inc(sem["fin%d" % k], 1)
    g.sync.wait_ge(sem.fin0, 1)
    g.sync.dma_start(blk(T.y, src[0]), blk(T.yb, src[0])).then_inc(sem.st, 16)
    act.wait_ge(sem.fin1, 1)
    act.dma_start(blk(T.y, src[1]), blk(T.yb, src[1])).then_inc(sem.st2, 16)

    ublock(N - 2)
    g.sync.wait_ge(sem.st, 16 * (N - 2))
    act.wait_ge(sem.st2, 16)
